import numpy as np
import ml_dtypes


def mxq(x, axis, fmt="e4m3"):
    dtype, down = {"e4m3": (ml_dtypes.float8_e4m3fn, 7), "e5m2": (ml_dtypes.float8_e5m2, 14)}[fmt]
    v = np.moveaxis(np.asarray(x, np.float32).astype(ml_dtypes.bfloat16).astype(np.float64), axis, -1)
    blocks = v.reshape(v.shape[:-1] + (-1, 32))
    amax = np.abs(blocks).max(-1, keepdims=True)
    byte = np.maximum(np.where(amax > 0, np.frexp(amax)[1] - 1 + 127, 0) - down, 1)
    scale = np.exp2(byte - 127.0)
    codes = (blocks / scale).astype(np.float32).astype(dtype).astype(np.float64)
    return np.moveaxis((codes * scale).reshape(v.shape), -1, axis)


WIDE = False


def mx_kscale(k):
    if not WIDE:
        return np.ones(k)
    levels = np.array([10, -10, 5, -5, 0])
    if k % 512:
        return np.exp2(np.random.permutation(np.resize(levels, k // 32))).repeat(32)
    a = np.empty((k // 512, 16))
    for p in range(k // 512):
        a[p, :8] = np.random.permutation(np.resize(levels, 8))
        for g in range(8):
            far = levels[np.abs(levels - a[p, g]) >= 10]
            a[p, g + 8] = far[np.random.randint(len(far))]
    return np.exp2(a.ravel()).repeat(32)


def f64(x):
    return np.asarray(x).astype(np.float64)


def striped(idx):
    return np.tile(idx.reshape(-1, 16).T, (8, 1)).astype(np.uint16)


def unstriped(offs):
    return offs[:16].T.reshape(-1).astype(np.int64)


E2M1 = np.array([0.0, 0.5, 1.0, 1.5, 2.0, 3.0, 4.0, 6.0, -0.0, -0.5, -1.0, -1.5, -2.0, -3.0, -4.0, -6.0])


def pack_fp4(w):
    k, n = w.shape
    w = f64(np.asarray(w, np.float32).astype(ml_dtypes.bfloat16)).reshape(k // 32, 32, n)
    amax = np.abs(w).max(1)
    mant, ex = np.frexp(amax / 6.0)
    byte = np.clip(np.where(amax > 0, np.where(mant > 0.5, ex, ex - 1) + 127, 1), 1, 254)
    scaled = (w * np.exp2(127.0 - byte)[:, None, :]).reshape(k, n).astype(np.float32)
    c = np.ascontiguousarray(scaled.reshape(k // 512, 128, 4, n).transpose(0, 1, 3, 2)).astype(ml_dtypes.float4_e2m1fn).view(np.uint8) & 0xF
    words = (c[..., 0::2] | (c[..., 1::2] << 4)).reshape(k // 512, 128, 2 * n)
    return np.ascontiguousarray(words), np.ascontiguousarray(byte.astype(np.uint8).reshape(k // 512, 16, n))


def unpack_fp4(words, scales):
    g, _, n = scales.shape
    words = np.ascontiguousarray(words).reshape(g, 128, n, 2)
    nib = np.empty((g, 128, n, 4), np.uint8)
    nib[..., 0::2] = words & 0xF
    nib[..., 1::2] = words >> 4
    vals = E2M1[nib] * np.repeat(np.exp2(scales.astype(np.float64) - 127.0), 8, axis=1)[..., None]
    return vals.transpose(0, 1, 3, 2).reshape(g * 512, n)


def relu(v):
    return np.maximum(v, 0.0)


K, T, S, H, N, U, V = 1024, 2048, 1024, 512, 128, 1024, 512


def setup_inputs():
    n = np.random.standard_normal
    s = mx_kscale(K)[:, None]
    u = mx_kscale(H)
    packed_w3 = pack_fp4(n((H, N)) / np.sqrt(H) / u[:, None])
    return {
        "xT": (n((K, T)) * s).astype(np.float32),
        "w1": (n((K, H)) / np.sqrt(K) / s * u).astype(np.float32),
        "w2": (n((K, H)) / np.sqrt(K) / s * u).astype(np.float32),
        "w3_words": packed_w3[0],
        "w3_scales": packed_w3[1],
        "offs": striped(np.random.permutation(T)[:S]),
        "near": striped(np.random.permutation(U)[:V]),
        "far": striped(np.random.permutation(U)[:V]),
    }


def reference(xT, w1, w2, w3_words, w3_scales, offs, near, far):
    xq = mxq(f64(xT)[:, unstriped(offs)], 0, "e4m3")
    a = np.zeros((H, S))
    a[:, unstriped(near)] = relu(mxq(f64(w1), 0, "e4m3").T @ xq[:, :V])
    e = np.zeros((H, S))
    e[:, unstriped(far)] = relu(mxq(f64(w2), 0, "e4m3").T @ xq[:, V:2 * V])
    z = np.maximum(a, e)
    return unpack_fp4(w3_words, w3_scales).T @ mxq(z, 0, "e4m3")

@@ -1,0 +1,192 @@
+from contextlib import ExitStack
+
+import concourse.mybir as mybir
+
+K, T, S, H, N, V = 1024, 2048, 1024, 512, 128, 512
+FLOPS = 2 * (2 * K * H * V + H * N * S)
+
+F32 = mybir.dt.float32
+BF16 = mybir.dt.bfloat16
+I32 = mybir.dt.int32
+U32 = mybir.dt.uint32
+U16 = mybir.dt.uint16
+U8 = mybir.dt.uint8
+FP8X4 = mybir.dt.float8_e4m3fn_x4
+FP4X4 = mybir.dt.float4_e2m1fn_x4
+MAX = mybir.AluOpType.max
+
+P = 128
+PACK = 4
+K_PASS = P * PACK
+LIST_COLS = V // 16
+
+
+def tile_picked_bev_max_e_kernel(tc, xT, w1, w2, w3_words, w3_scales, offs, near, far, out):
+    nc = tc.nc
+    with ExitStack() as ctx:
+        lists = ctx.enter_context(tc.tile_pool(name="lists", bufs=1))
+        sb = ctx.enter_context(tc.tile_pool(name="sb", bufs=1))
+        psum = ctx.enter_context(tc.psum_pool(name="psum", bufs=1))
+
+        def tile(name, shape, dtype, tag=None):
+            return sb.tile(shape, dtype, name=name, tag=tag or name, align_bytes=64)
+
+        offs_sb = lists.tile([P, S // 16], U16, name="offs_sb")
+        near_sb = lists.tile([P, LIST_COLS], U16, name="near_sb")
+        far_sb = lists.tile([P, LIST_COLS], U16, name="far_sb")
+        cells_of = [near_sb, far_sb]
+
+        x_rows = xT.rearrange("(g p j) t -> g j p t", p=P, j=PACK)
+        x_plane = {}
+        w_raw = {}
+
+        def load_x(g, j):
+            x_plane[g, j] = tile(f"x{g}{j}", [P, T], F32)
+            nc.sync.dma_start(x_plane[g, j][:], x_rows[g, j])
+
+        def load_w(s, g):
+            w_raw[s, g] = tile(f"wraw{s}{g}", [P, PACK, H], F32)
+            nc.sync.dma_start(w_raw[s, g][:], (w1, w2)[s].rearrange("(g p j) c -> g p j c", p=P, j=PACK)[g])
+
+        load_x(0, 0)
+        nc.sync.dma_start(offs_sb[:], offs)
+        for j in range(1, PACK):
+            load_x(0, j)
+        load_x(1, 0)
+        load_x(1, 1)
+        load_w(0, 0)
+        load_x(1, 2)
+        load_x(1, 3)
+        load_w(0, 1)
+        nc.sync.dma_start(near_sb[:], near)
+        load_w(1, 0)
+        load_w(1, 1)
+        nc.sync.dma_start(far_sb[:], far)
+        w3_sb = tile("w3_sb", [P, 2 * N], U8)
+        nc.sync.dma_start(w3_sb[:].bitcast(I32), w3_words[0].bitcast(I32))
+        w3_scale = tile("w3_scale", [P, N], U8)
+        nc.gpsimd.memset(w3_scale[:], 0)
+        for q in range(4):
+            nc.sync.dma_start(w3_scale[32 * q : 32 * q + 4, :].bitcast(I32), w3_scales[0, 4 * q : 4 * q + 4, :].bitcast(I32))
+
+        cell_map = {}
+        for s in range(2):
+            for t in range(PACK):
+                cell_map[s, t] = tile(f"map{s}{t}", [P, S], F32)
+                if s == 0 and t < 3:
+                    nc.vector.memset(cell_map[s, t][:], 0.0)
+                else:
+                    nc.scalar.copy(cell_map[s, t][:], cell_map[0, 0][:])
+
+        def quantize(name, woven, width):
+            codes = tile(name + "_codes", [P, width], U32)
+            scales = tile(name + "_scales", [P, width], U8)
+            nc.vector.quantize_mx(out=codes[:].bitcast(FP8X4), scales=scales[:], in_=woven)
+            return codes, scales
+
+        def weave(engine_copy, dst, src):
+            engine_copy(dst.rearrange("p (c i) j -> p c j i", i=4), src.rearrange("p j (c i) -> p c j i", i=4))
+
+        def weave_w(engine_copy, dst, src):
+            engine_copy(
+                dst.rearrange("p t (a i) j -> p a j i t", i=2),
+                src.rearrange("p j (a i t) -> p a j i t", i=2, t=PACK),
+            )
+
+        x_woven = {(s, g): tile(f"xw{s}{g}", [P, V, PACK], BF16) for s, g in ((0, 0), (1, 0))}
+        flat = lambda woven: woven[:].rearrange("p c j -> p (c j)")
+        xq, wq = {}, {}
+
+        picked0 = tile("picked0", [P, PACK, S], BF16)
+        for j in range(PACK):
+            nc.vector.tensor_copy(picked0[:, j, :], x_plane[0, j][:].indirect(offs_sb[:]))
+        for s in range(2):
+            weave(nc.scalar.copy, x_woven[s, 0][:], picked0[:, :, s * V : (s + 1) * V])
+        picked1 = tile("picked1", [P, PACK, S], BF16)
+        for j in range(2):
+            nc.vector.tensor_copy(picked1[:, j, :], x_plane[1, j][:].indirect(offs_sb[:]))
+            xq[j, 0] = quantize(f"xq{j}0", flat(x_woven[j, 0]), V)
+        w_woven = {(s, g): tile(f"ww{s}{g}", [P, PACK, P, PACK], BF16) for s in range(2) for g in range(2)}
+        wflat = lambda woven: woven.rearrange("p t m j -> p (t m j)")
+        weave_w(nc.scalar.copy, w_woven[0, 0][:], w_raw[0, 0][:])
+        far_offs = offs_sb[:, LIST_COLS : 2 * LIST_COLS]
+        nc.vector.tensor_copy(picked1[:, 2, V:S], x_plane[1, 2][:].indirect(far_offs))
+        wq[0, 0] = quantize("wq00", wflat(w_woven[0, 0][:]), H)
+        x_woven[0, 1] = tile("xw01", [P, V, PACK], BF16, tag="wraw00")
+        weave(nc.scalar.copy, x_woven[0, 1][:, :, 0:2], picked1[:, 0:2, 0:V])
+        for j in range(2, PACK):
+            nc.vector.tensor_copy(x_woven[0, 1][:, :, j], x_plane[1, j][:].indirect(offs_sb[:, 0:LIST_COLS]))
+        xq[0, 1] = quantize("xq01", flat(x_woven[0, 1]), V)
+
+        def lhs(s, g, t):
+            if (s, g) == (0, 1):
+                codes, scales = wq[0, 1, t]
+                return codes[:].bitcast(FP8X4), scales[:]
+            codes, scales = wq[s, g]
+            return codes[:, t * P : (t + 1) * P].bitcast(FP8X4), scales[:, t * P : (t + 1) * P]
+
+        acc = {}
+
+        def product(s, g, t):
+            if g == 0:
+                acc[s, t] = psum.tile([P, V], F32, name=f"acc{s}{t}", tag=f"bank{4 * s + t}")
+            w_codes, w_scales = lhs(s, g, t)
+            x_codes, x_scales = xq[s, g]
+            nc.tensor.matmul_mx(out=acc[s, t][:], lhsT=w_codes, lhsT_scale=w_scales, rhs=x_codes[:].bitcast(FP8X4),
+                                rhs_scale=x_scales[:], start=(g == 0), stop=(g == 1))
+
+        def scatter(s, t, tag=None):
+            staged = tile(f"staged{s}{t}", [P, V], F32, tag)
+            nc.scalar.copy(staged[:], acc[s, t][:])
+            nc.vector.tensor_copy(cell_map[s, t][:].indirect(cells_of[s][:]), staged[:])
+
+        for t in range(PACK):
+            product(0, 0, t)
+        w1_by_t = w_raw[0, 1][:].rearrange("p j (m t) -> p t m j", t=PACK)
+        for t in range(PACK):
+            piece = picked1[:, 3, V:S] if t == 0 else w_woven[0, 1][:, t].rearrange("p m j -> p (m j)")
+            nc.scalar.copy(piece.rearrange("p (m j) -> p m j", j=PACK), w1_by_t[:, t])
+            wq[0, 1, t] = quantize(f"wq01{t}", piece, P)
+            product(0, 1, t)
+            if t == 0:
+                nc.vector.tensor_copy(picked1[:, 3, V:S], x_plane[1, 3][:].indirect(far_offs))
+        scatter(0, 0)
+        scatter(0, 1)
+        x_woven[1, 1] = tile("xw11", [P, V, PACK], BF16, tag="wraw01")
+        weave(nc.scalar.copy, x_woven[1, 1][:], picked1[:, :, V:S])
+        xq[1, 1] = quantize("xq11", flat(x_woven[1, 1]), V)
+        for g in range(2):
+            weave_w(nc.scalar.copy, w_woven[1, g][:], w_raw[1, g][:])
+            wq[1, g] = quantize(f"wq1{g}", wflat(w_woven[1, g][:]), H)
+            for t in range(PACK):
+                product(1, g, t)
+            scatter(0, 2 + g, tag=f"wraw1{g}")
+
+        halves = [slice(0, V), slice(V, S)]
+        z_low = tile("z_low", [P, 2, S], BF16)
+        z_high = [tile(f"z_high{h}", [P, 2, V], BF16) for h in range(2)]
+        z_woven = [tile(f"z_woven{h}", [P, V, PACK], BF16, tag=f"x0{h}") for h in range(2)]
+
+        def join(dst, t, cols):
+            nc.vector.scalar_tensor_tensor(dst, cell_map[0, t][:, cols], 0.0, cell_map[1, t][:, cols], MAX, MAX)
+
+        for t in range(PACK):
+            scatter(1, t)
+            if t < 2:
+                join(z_low[:, t, :], t, slice(0, S))
+        for h in (1, 0):
+            weave(nc.scalar.copy, z_woven[h][:, :, 0:2], z_low[:, :, halves[h]])
+        for h in (1, 0):
+            join(z_high[h][:, 0, :], 2, halves[h])
+            join(z_high[h][:, 1, :], 3, halves[h])
+            weave((nc.vector.tensor_copy, nc.scalar.copy)[h], z_woven[h][:, :, 2:4], z_high[h][:])
+        quarter = V // 2
+        for n, (h, u) in enumerate(((0, 0), (0, 1), (1, 0), (1, 1))):
+            z_in = z_woven[h][:, u * quarter : (u + 1) * quarter, :].rearrange("p c j -> p (c j)")
+            z_codes, z_scales = quantize(f"zq{n}", z_in, quarter)
+            res = psum.tile([P, quarter], F32, name=f"res{n}", tag=f"bank{n}")
+            nc.tensor.matmul_mx(out=res[:], lhsT=w3_sb[:].bitcast(FP4X4), lhsT_scale=w3_scale[:], rhs=z_codes[:].bitcast(FP8X4),
+                                rhs_scale=z_scales[:], start=True, stop=True)
+            result = tile(f"result{n}", [P, quarter], F32, tag=f"x1{n}")
+            (nc.scalar.copy, nc.vector.tensor_copy)[n == PACK - 1](result[:], res[:])
+            nc.sync.dma_start(out[:, n * quarter : (n + 1) * quarter], result[:])

@@ -14,6 +14,9 @@ U8 = mybir.dt.uint8
 FP8X4 = mybir.dt.float8_e4m3fn_x4
 FP4X4 = mybir.dt.float4_e2m1fn_x4
 MAX = mybir.AluOpType.max
+ADD = mybir.AluOpType.add
+SUB = mybir.AluOpType.subtract
+RELU = mybir.ActivationFunctionType.Relu
 
 P = 128
 PACK = 4
@@ -76,7 +79,7 @@ def tile_picked_bev_max_e_kernel(tc, xT, w1, w2, w3_words, w3_scales, offs, near
                 if s == 0 and t < 3:
                     nc.vector.memset(cell_map[s, t][:], 0.0)
                 else:
-                    nc.scalar.copy(cell_map[s, t][:], cell_map[0, 0][:])
+                    nc.scalar.activation(cell_map[s, t][:], cell_map[0, 0][:], RELU)
 
         def quantize(name, woven, width):
             codes = tile(name + "_codes", [P, width], U32)
@@ -119,8 +122,8 @@ def tile_picked_bev_max_e_kernel(tc, xT, w1, w2, w3_words, w3_scales, offs, near
         xq[0, 1] = quantize("xq01", flat(x_woven[0, 1]), V)
 
         def lhs(s, g, t):
-            if (s, g) == (0, 1):
-                codes, scales = wq[0, 1, t]
+            if g == 1:
+                codes, scales = wq[s, 1, t]
                 return codes[:].bitcast(FP8X4), scales[:]
             codes, scales = wq[s, g]
             return codes[:, t * P : (t + 1) * P].bitcast(FP8X4), scales[:, t * P : (t + 1) * P]
@@ -137,7 +140,10 @@ def tile_picked_bev_max_e_kernel(tc, xT, w1, w2, w3_words, w3_scales, offs, near
 
         def scatter(s, t, tag=None):
             staged = tile(f"staged{s}{t}", [P, V], F32, tag)
-            nc.scalar.copy(staged[:], acc[s, t][:])
+            if s == 0:
+                nc.scalar.activation(staged[:], acc[s, t][:], RELU)
+            else:
+                nc.scalar.copy(staged[:], acc[s, t][:])
             nc.vector.tensor_copy(cell_map[s, t][:].indirect(cells_of[s][:]), staged[:])
 
         for t in range(PACK):
@@ -155,12 +161,17 @@ def tile_picked_bev_max_e_kernel(tc, xT, w1, w2, w3_words, w3_scales, offs, near
         x_woven[1, 1] = tile("xw11", [P, V, PACK], BF16, tag="wraw01")
         weave(nc.scalar.copy, x_woven[1, 1][:], picked1[:, :, V:S])
         xq[1, 1] = quantize("xq11", flat(x_woven[1, 1]), V)
-        for g in range(2):
-            weave_w(nc.scalar.copy, w_woven[1, g][:], w_raw[1, g][:])
-            wq[1, g] = quantize(f"wq1{g}", wflat(w_woven[1, g][:]), H)
-            for t in range(PACK):
-                product(1, g, t)
-            scatter(0, 2 + g, tag=f"wraw1{g}")
+        weave_w(nc.scalar.copy, w_woven[1, 0][:], w_raw[1, 0][:])
+        wq[1, 0] = quantize("wq10", wflat(w_woven[1, 0][:]), H)
+        for t in range(PACK):
+            product(1, 0, t)
+        w2_by_t = w_raw[1, 1][:].rearrange("p j (m t) -> p t m j", t=PACK)
+        for t in range(PACK):
+            nc.scalar.copy(w_woven[1, 1][:, t], w2_by_t[:, t])
+            wq[1, 1, t] = quantize(f"wq11{t}", w_woven[1, 1][:, t].rearrange("p m j -> p (m j)"), P)
+            product(1, 1, t)
+            if t == 0:
+                scatter(0, 2, tag="wraw10")
 
         halves = [slice(0, V), slice(V, S)]
         z_low = tile("z_low", [P, 2, S], BF16)
@@ -168,18 +179,31 @@ def tile_picked_bev_max_e_kernel(tc, xT, w1, w2, w3_words, w3_scales, offs, near
         z_woven = [tile(f"z_woven{h}", [P, V, PACK], BF16, tag=f"x0{h}") for h in range(2)]
 
         def join(dst, t, cols):
-            nc.vector.scalar_tensor_tensor(dst, cell_map[0, t][:, cols], 0.0, cell_map[1, t][:, cols], MAX, MAX)
+            nc.vector.tensor_tensor(dst, cell_map[0, t][:, cols], cell_map[1, t][:, cols], MAX)
+
+        def join_by_sums(dsts, t, which, tag):
+            work = tile(f"work{t}", [P, 2, S], F32, tag=tag)
+            for h in which:
+                nc.gpsimd.tensor_tensor(work[:, 0, halves[h]], cell_map[1, t][:, halves[h]], cell_map[0, t][:, halves[h]], SUB)
+                nc.scalar.activation(work[:, 1, halves[h]], work[:, 0, halves[h]], RELU)
+            for h in which:
+                nc.gpsimd.tensor_tensor(dsts[h], work[:, 1, halves[h]], cell_map[0, t][:, halves[h]], ADD)
 
         for t in range(PACK):
             scatter(1, t)
-            if t < 2:
-                join(z_low[:, t, :], t, slice(0, S))
-        for h in (1, 0):
+        scatter(0, 3, tag="staged10")
+        for t in range(2):
+            join_by_sums([z_low[:, t, halves[h]] for h in range(2)], t, (0, 1), f"x0{2 + t}")
+        join_by_sums([None, z_high[1][:, 0, :]], 2, (1,), "picked0")
+        for h in range(2):
             weave(nc.scalar.copy, z_woven[h][:, :, 0:2], z_low[:, :, halves[h]])
+        join(z_high[0][:, 0, :], 2, halves[0])
         for h in (1, 0):
-            join(z_high[h][:, 0, :], 2, halves[h])
             join(z_high[h][:, 1, :], 3, halves[h])
-            weave((nc.vector.tensor_copy, nc.scalar.copy)[h], z_woven[h][:, :, 2:4], z_high[h][:])
+        for u in range(2):
+            cols = slice(u * V // 2, (u + 1) * V // 2)
+            weave(nc.scalar.copy, z_woven[1][:, cols, 2:4], z_high[1][:, :, cols])
+        weave(nc.vector.tensor_copy, z_woven[0][:, :, 2:4], z_high[0][:])
         quarter = V // 2
         for n, (h, u) in enumerate(((0, 0), (0, 1), (1, 0), (1, 1))):
             z_in = z_woven[h][:, u * quarter : (u + 1) * quarter, :].rearrange("p c j -> p (c j)")

@@ -15,6 +15,8 @@ FP8X4 = mybir.dt.float8_e4m3fn_x4
 FP4X4 = mybir.dt.float4_e2m1fn_x4
 MAX = mybir.AluOpType.max
 ADD = mybir.AluOpType.add
+MULT = mybir.AluOpType.mult
+COPY = mybir.ActivationFunctionType.Copy
 SUB = mybir.AluOpType.subtract
 RELU = mybir.ActivationFunctionType.Relu
 
@@ -81,8 +83,8 @@ def tile_picked_bev_max_e_kernel(tc, xT, w1, w2, w3_words, w3_scales, offs, near
                 else:
                     nc.scalar.activation(cell_map[s, t][:], cell_map[0, 0][:], RELU)
 
-        def quantize(name, woven, width):
-            codes = tile(name + "_codes", [P, width], U32)
+        def quantize(name, woven, width, tag=None):
+            codes = tile(name + "_codes", [P, width], U32, tag)
             scales = tile(name + "_scales", [P, width], U8)
             nc.vector.quantize_mx(out=codes[:].bitcast(FP8X4), scales=scales[:], in_=woven)
             return codes, scales
@@ -90,42 +92,50 @@ def tile_picked_bev_max_e_kernel(tc, xT, w1, w2, w3_words, w3_scales, offs, near
         def weave(engine_copy, dst, src):
             engine_copy(dst.rearrange("p (c i) j -> p c j i", i=4), src.rearrange("p j (c i) -> p c j i", i=4))
 
+        def weave_pair(engine_copy, dst, src):
+            engine_copy(dst, src.rearrange("p j c -> p c j"))
+
         def weave_w(engine_copy, dst, src):
             engine_copy(
                 dst.rearrange("p t (a i) j -> p a j i t", i=2),
                 src.rearrange("p j (a i t) -> p a j i t", i=2, t=PACK),
             )
 
-        x_woven = {(s, g): tile(f"xw{s}{g}", [P, V, PACK], BF16) for s, g in ((0, 0), (1, 0))}
+        x_woven = {(s, 0): tile(f"xw{s}0", [P, V, PACK], BF16) for s in range(2)}
         flat = lambda woven: woven[:].rearrange("p c j -> p (c j)")
         xq, wq = {}, {}
 
         picked0 = tile("picked0", [P, PACK, S], BF16)
         for j in range(PACK):
             nc.vector.tensor_copy(picked0[:, j, :], x_plane[0, j][:].indirect(offs_sb[:]))
-        for s in range(2):
-            weave(nc.scalar.copy, x_woven[s, 0][:], picked0[:, :, s * V : (s + 1) * V])
+            if j % 2:
+                for s in range(2):
+                    weave_pair(nc.scalar.copy, x_woven[s, 0][:, :, j - 1 : j + 1], picked0[:, j - 1 : j + 1, s * V : (s + 1) * V])
         picked1 = tile("picked1", [P, PACK, S], BF16)
         for j in range(2):
             nc.vector.tensor_copy(picked1[:, j, :], x_plane[1, j][:].indirect(offs_sb[:]))
-            xq[j, 0] = quantize(f"xq{j}0", flat(x_woven[j, 0]), V)
-        w_woven = {(s, g): tile(f"ww{s}{g}", [P, PACK, P, PACK], BF16) for s in range(2) for g in range(2)}
+            xq[j, 0] = quantize(f"xq{j}0", flat(x_woven[j, 0]), V, f"x1{j}")
+        w_woven = {(s, g): tile(f"ww{s}{g}", [P, PACK, P, PACK], BF16) for s, g in ((0, 0),)}
         wflat = lambda woven: woven.rearrange("p t m j -> p (t m j)")
         weave_w(nc.scalar.copy, w_woven[0, 0][:], w_raw[0, 0][:])
         far_offs = offs_sb[:, LIST_COLS : 2 * LIST_COLS]
-        nc.vector.tensor_copy(picked1[:, 2, V:S], x_plane[1, 2][:].indirect(far_offs))
         wq[0, 0] = quantize("wq00", wflat(w_woven[0, 0][:]), H)
-        x_woven[0, 1] = tile("xw01", [P, V, PACK], BF16, tag="wraw00")
-        weave(nc.scalar.copy, x_woven[0, 1][:, :, 0:2], picked1[:, 0:2, 0:V])
+        x12_bf16 = tile("x12_bf16", [P, T], BF16, tag="ww00")
+        nc.gpsimd.tensor_scalar(x12_bf16[:], x_plane[1, 2][:], 1.0, 0.0, MULT, ADD)
+        x_woven1 = tile("xw1", [P, 2, V, PACK], BF16, tag="wraw00")
+        for s in range(2):
+            x_woven[s, 1] = x_woven1[:, s]
+            weave_pair(nc.scalar.copy, x_woven[s, 1][:, :, 0:2], picked1[:, 0:2, s * V : (s + 1) * V])
         for j in range(2, PACK):
             nc.vector.tensor_copy(x_woven[0, 1][:, :, j], x_plane[1, j][:].indirect(offs_sb[:, 0:LIST_COLS]))
         xq[0, 1] = quantize("xq01", flat(x_woven[0, 1]), V)
 
         def lhs(s, g, t):
             if g == 1:
-                codes, scales = wq[s, 1, t]
-                return codes[:].bitcast(FP8X4), scales[:]
-            codes, scales = wq[s, g]
+                codes, scales = wq[s, 1, t // 2]
+                t = t % 2
+            else:
+                codes, scales = wq[s, g]
             return codes[:, t * P : (t + 1) * P].bitcast(FP8X4), scales[:, t * P : (t + 1) * P]
 
         acc = {}
@@ -138,79 +148,98 @@ def tile_picked_bev_max_e_kernel(tc, xT, w1, w2, w3_words, w3_scales, offs, near
             nc.tensor.matmul_mx(out=acc[s, t][:], lhsT=w_codes, lhsT_scale=w_scales, rhs=x_codes[:].bitcast(FP8X4),
                                 rhs_scale=x_scales[:], start=(g == 0), stop=(g == 1))
 
-        def scatter(s, t, tag=None):
-            staged = tile(f"staged{s}{t}", [P, V], F32, tag)
+        def scatter(s, t, tag=None, part=slice(0, V)):
+            staged = tile(f"staged{s}{t}_{part.start}", [P, part.stop - part.start], F32, tag)
             if s == 0:
-                nc.scalar.activation(staged[:], acc[s, t][:], RELU)
+                nc.scalar.activation(staged[:], acc[s, t][:, part], RELU)
             else:
-                nc.scalar.copy(staged[:], acc[s, t][:])
-            nc.vector.tensor_copy(cell_map[s, t][:].indirect(cells_of[s][:]), staged[:])
+                nc.scalar.copy(staged[:], acc[s, t][:, part])
+            nc.vector.tensor_copy(cell_map[s, t][:].indirect(cells_of[s][:, part.start // 16 : part.stop // 16]), staged[:])
 
         for t in range(PACK):
             product(0, 0, t)
-        w1_by_t = w_raw[0, 1][:].rearrange("p j (m t) -> p t m j", t=PACK)
-        for t in range(PACK):
-            piece = picked1[:, 3, V:S] if t == 0 else w_woven[0, 1][:, t].rearrange("p m j -> p (m j)")
-            nc.scalar.copy(piece.rearrange("p (m j) -> p m j", j=PACK), w1_by_t[:, t])
-            wq[0, 1, t] = quantize(f"wq01{t}", piece, P)
-            product(0, 1, t)
-            if t == 0:
-                nc.vector.tensor_copy(picked1[:, 3, V:S], x_plane[1, 3][:].indirect(far_offs))
+
+        def weave_w_half(s, u, dst):
+            src = w_raw[s, 1][:].rearrange("p j (m t) -> p m t j", t=PACK)[:, :, 2 * u : 2 * u + 2, :]
+            nc.scalar.copy(dst.rearrange("p (t m j) -> p m t j", t=2, j=PACK), src)
+            wq[s, 1, u] = quantize(f"wq{s}1{u}", dst, 2 * P)
+
+        weave_w_half(0, 0, picked1[:, 3, :])
+        product(0, 1, 0)
+        nc.vector.tensor_copy(picked1[:, 3, V:S], x_plane[1, 3][:].indirect(far_offs))
         scatter(0, 0)
+        product(0, 1, 1)
+        weave_w_half(0, 1, picked1[:, 2, :])
+        product(0, 1, 2)
+        product(0, 1, 3)
         scatter(0, 1)
-        x_woven[1, 1] = tile("xw11", [P, V, PACK], BF16, tag="wraw01")
-        weave(nc.scalar.copy, x_woven[1, 1][:], picked1[:, :, V:S])
+        nc.scalar.activation(picked1[:, 2, V:S], x12_bf16[:].indirect(far_offs), COPY)
+        weave_pair(nc.scalar.copy, x_woven[1, 1][:, :, 2:4], picked1[:, 2:4, V:S])
         xq[1, 1] = quantize("xq11", flat(x_woven[1, 1]), V)
+        w_woven[1, 0] = tile("ww10", [P, PACK, P, PACK], BF16, tag="ww00")
         weave_w(nc.scalar.copy, w_woven[1, 0][:], w_raw[1, 0][:])
         wq[1, 0] = quantize("wq10", wflat(w_woven[1, 0][:]), H)
         for t in range(PACK):
             product(1, 0, t)
-        w2_by_t = w_raw[1, 1][:].rearrange("p j (m t) -> p t m j", t=PACK)
-        for t in range(PACK):
-            nc.scalar.copy(w_woven[1, 1][:, t], w2_by_t[:, t])
-            wq[1, 1, t] = quantize(f"wq11{t}", w_woven[1, 1][:, t].rearrange("p m j -> p (m j)"), P)
-            product(1, 1, t)
-            if t == 0:
+        for u in range(2):
+            half_woven = tile(f"ww11{u}", [P, 2 * V], BF16, tag=("picked1", "ww00")[u])
+            weave_w_half(1, u, half_woven[:])
+            product(1, 1, 2 * u)
+            product(1, 1, 2 * u + 1)
+            if u == 0:
                 scatter(0, 2, tag="wraw10")
 
         halves = [slice(0, V), slice(V, S)]
         z_low = tile("z_low", [P, 2, S], BF16)
-        z_high = [tile(f"z_high{h}", [P, 2, V], BF16) for h in range(2)]
-        z_woven = [tile(f"z_woven{h}", [P, V, PACK], BF16, tag=f"x0{h}") for h in range(2)]
 
         def join(dst, t, cols):
             nc.vector.tensor_tensor(dst, cell_map[0, t][:, cols], cell_map[1, t][:, cols], MAX)
 
-        def join_by_sums(dsts, t, which, tag):
-            work = tile(f"work{t}", [P, 2, S], F32, tag=tag)
-            for h in which:
-                nc.gpsimd.tensor_tensor(work[:, 0, halves[h]], cell_map[1, t][:, halves[h]], cell_map[0, t][:, halves[h]], SUB)
-                nc.scalar.activation(work[:, 1, halves[h]], work[:, 0, halves[h]], RELU)
-            for h in which:
-                nc.gpsimd.tensor_tensor(dsts[h], work[:, 1, halves[h]], cell_map[0, t][:, halves[h]], ADD)
+        work = {}
+        work_tag = {(0, 0): "x02", (0, 1): "picked0", (1, 0): "x12", (1, 1): "x03", (2, 1): "x13"}
+        diff_tag = {(0, 0): "xw00", (0, 1): "xw10", (1, 0): "x02", (1, 1): "xw10", (2, 1): "x12"}
+
+        def excess(t, h):
+            diff = tile(f"diff{t}{h}", [P, V], F32, tag=diff_tag[t, h])
+            work[t, h] = tile(f"work{t}{h}", [P, V], F32, tag=work_tag[t, h])
+            nc.gpsimd.tensor_tensor(diff[:], cell_map[1, t][:, halves[h]], cell_map[0, t][:, halves[h]], SUB)
+            nc.scalar.activation(work[t, h][:], diff[:], RELU)
+
+        def add_back(dst, t, h):
+            nc.gpsimd.tensor_tensor(dst, work[t, h][:], cell_map[0, t][:, halves[h]], ADD)
 
         for t in range(PACK):
             scatter(1, t)
-        scatter(0, 3, tag="staged10")
         for t in range(2):
-            join_by_sums([z_low[:, t, halves[h]] for h in range(2)], t, (0, 1), f"x0{2 + t}")
-        join_by_sums([None, z_high[1][:, 0, :]], 2, (1,), "picked0")
+            for h in range(2):
+                excess(t, h)
+            add_back(z_low[:, t, halves[0]], t, 0)
+            if t == 1:
+                excess(2, 1)
+            add_back(z_low[:, t, halves[1]], t, 1)
+            if t == 0:
+                scatter(0, 3, tag="picked0")
+        z_high_both = tile("z_high", [P, 2, 2, V], BF16, tag="x03")
+        z_high = [z_high_both[:, h] for h in range(2)]
+        add_back(z_high[1][:, 0, :], 2, 1)
+        z_woven = [tile(f"z_woven{h}", [P, V, PACK], BF16, tag=("x00", "x12")[h]) for h in range(2)]
         for h in range(2):
-            weave(nc.scalar.copy, z_woven[h][:, :, 0:2], z_low[:, :, halves[h]])
+            weave_pair(nc.scalar.copy, z_woven[h][:, :, 0:2], z_low[:, :, halves[h]])
         join(z_high[0][:, 0, :], 2, halves[0])
-        for h in (1, 0):
+        for h in range(2):
             join(z_high[h][:, 1, :], 3, halves[h])
-        for u in range(2):
-            cols = slice(u * V // 2, (u + 1) * V // 2)
-            weave(nc.scalar.copy, z_woven[1][:, cols, 2:4], z_high[1][:, :, cols])
-        weave(nc.vector.tensor_copy, z_woven[0][:, :, 2:4], z_high[0][:])
+        for h in range(2):
+            for u in range(2):
+                cols = slice(u * V // 2, (u + 1) * V // 2)
+                weave_pair((nc.vector.tensor_copy, nc.scalar.copy)[h], z_woven[h][:, cols, 2:4], z_high[h][:, :, cols])
         quarter = V // 2
+        result = tile("result", [P, S], F32, tag="x03")
         for n, (h, u) in enumerate(((0, 0), (0, 1), (1, 0), (1, 1))):
             z_in = z_woven[h][:, u * quarter : (u + 1) * quarter, :].rearrange("p c j -> p (c j)")
             z_codes, z_scales = quantize(f"zq{n}", z_in, quarter)
             res = psum.tile([P, quarter], F32, name=f"res{n}", tag=f"bank{n}")
             nc.tensor.matmul_mx(out=res[:], lhsT=w3_sb[:].bitcast(FP4X4), lhsT_scale=w3_scale[:], rhs=z_codes[:].bitcast(FP8X4),
                                 rhs_scale=z_scales[:], start=True, stop=True)
-            result = tile(f"result{n}", [P, quarter], F32, tag=f"x1{n}")
-            (nc.scalar.copy, nc.vector.tensor_copy)[n == PACK - 1](result[:], res[:])
-            nc.sync.dma_start(out[:, n * quarter : (n + 1) * quarter], result[:])
+            cols = slice(n * quarter, (n + 1) * quarter)
+            (nc.scalar.copy, nc.vector.tensor_copy)[n == PACK - 1](result[:, cols], res[:])
+            nc.sync.dma_start(out[:, cols], result[:, cols])

@@ -176,18 +176,20 @@ def tile_picked_bev_max_e_kernel(tc, xT, w1, w2, w3_words, w3_scales, offs, near
         nc.scalar.activation(picked1[:, 2, V:S], x12_bf16[:].indirect(far_offs), COPY)
         weave_pair(nc.scalar.copy, x_woven[1, 1][:, :, 2:4], picked1[:, 2:4, V:S])
         xq[1, 1] = quantize("xq11", flat(x_woven[1, 1]), V)
-        w_woven[1, 0] = tile("ww10", [P, PACK, P, PACK], BF16, tag="ww00")
+        first_half = tile("ww110", [P, 2 * V], BF16, tag="ww00")
+        weave_w_half(1, 0, first_half[:])
+        w_woven[1, 0] = tile("ww10", [P, PACK, P, PACK], BF16, tag="picked1")
         weave_w(nc.scalar.copy, w_woven[1, 0][:], w_raw[1, 0][:])
         wq[1, 0] = quantize("wq10", wflat(w_woven[1, 0][:]), H)
-        for t in range(PACK):
+        for t in range(2):
             product(1, 0, t)
-        for u in range(2):
-            half_woven = tile(f"ww11{u}", [P, 2 * V], BF16, tag=("picked1", "ww00")[u])
-            weave_w_half(1, u, half_woven[:])
-            product(1, 1, 2 * u)
-            product(1, 1, 2 * u + 1)
-            if u == 0:
-                scatter(0, 2, tag="wraw10")
+            product(1, 1, t)
+        scatter(0, 2, tag="wraw10")
+        second_half = tile("ww111", [P, 2 * V], BF16, tag="picked1")
+        weave_w_half(1, 1, second_half[:])
+        for t in range(2, PACK):
+            product(1, 0, t)
+            product(1, 1, t)
 
         halves = [slice(0, V), slice(V, S)]
         z_low = tile("z_low", [P, 2, S], BF16)
@@ -214,19 +216,16 @@ def tile_picked_bev_max_e_kernel(tc, xT, w1, w2, w3_words, w3_scales, offs, near
             for h in range(2):
                 excess(t, h)
             add_back(z_low[:, t, halves[0]], t, 0)
-            if t == 1:
-                excess(2, 1)
             add_back(z_low[:, t, halves[1]], t, 1)
             if t == 0:
                 scatter(0, 3, tag="picked0")
         z_high_both = tile("z_high", [P, 2, 2, V], BF16, tag="x03")
         z_high = [z_high_both[:, h] for h in range(2)]
-        add_back(z_high[1][:, 0, :], 2, 1)
-        z_woven = [tile(f"z_woven{h}", [P, V, PACK], BF16, tag=("x00", "x12")[h]) for h in range(2)]
+        z_woven = [tile(f"z_woven{h}", [P, V, PACK], BF16, tag=f"x0{h}") for h in range(2)]
         for h in range(2):
             weave_pair(nc.scalar.copy, z_woven[h][:, :, 0:2], z_low[:, :, halves[h]])
-        join(z_high[0][:, 0, :], 2, halves[0])
-        for h in range(2):
+        for h in (1, 0):
+            join(z_high[h][:, 0, :], 2, halves[h])
             join(z_high[h][:, 1, :], 3, halves[h])
         for h in range(2):
             for u in range(2):

@@ -1,6 +1,7 @@
 from contextlib import ExitStack
 
 import concourse.mybir as mybir
+from concourse.masks import make_identity
 
 K, T, S, H, N, V = 1024, 2048, 1024, 512, 128, 512
 FLOPS = 2 * (2 * K * H * V + H * N * S)
@@ -16,14 +17,19 @@ FP4X4 = mybir.dt.float4_e2m1fn_x4
 MAX = mybir.AluOpType.max
 ADD = mybir.AluOpType.add
 MULT = mybir.AluOpType.mult
-COPY = mybir.ActivationFunctionType.Copy
 SUB = mybir.AluOpType.subtract
+COPY = mybir.ActivationFunctionType.Copy
 RELU = mybir.ActivationFunctionType.Relu
 
 P = 128
 PACK = 4
-K_PASS = P * PACK
+NEAR, FAR = 0, 1
+SENSORS = (NEAR, FAR)
 LIST_COLS = V // 16
+HALF = S // 2
+QUARTER = S // 4
+MAPS_CLEARED_BY_VECTOR = 3
+TURNED_PLANE = 1
 
 
 def tile_picked_bev_max_e_kernel(tc, xT, w1, w2, w3_words, w3_scales, offs, near, far, out):
@@ -33,24 +39,26 @@ def tile_picked_bev_max_e_kernel(tc, xT, w1, w2, w3_words, w3_scales, offs, near
         sb = ctx.enter_context(tc.tile_pool(name="sb", bufs=1))
         psum = ctx.enter_context(tc.psum_pool(name="psum", bufs=1))
 
-        def tile(name, shape, dtype, tag=None):
-            return sb.tile(shape, dtype, name=name, tag=tag or name, align_bytes=64)
+        def tile(name, shape, dtype, after=None):
+            return sb.tile(shape, dtype, name=name, tag=after or name, align_bytes=64)
 
         offs_sb = lists.tile([P, S // 16], U16, name="offs_sb")
         near_sb = lists.tile([P, LIST_COLS], U16, name="near_sb")
         far_sb = lists.tile([P, LIST_COLS], U16, name="far_sb")
-        cells_of = [near_sb, far_sb]
+        cells_of = (near_sb, far_sb)
+        near_pillars = offs_sb[:, 0:LIST_COLS]
+        far_pillars = offs_sb[:, LIST_COLS : 2 * LIST_COLS]
+        pillars_of = (slice(0, V), slice(V, 2 * V))
 
         x_rows = xT.rearrange("(g p j) t -> g j p t", p=P, j=PACK)
-        x_plane = {}
-        w_raw = {}
+        x_plane, w_raw = {}, {}
 
         def load_x(g, j):
             x_plane[g, j] = tile(f"x{g}{j}", [P, T], F32)
             nc.sync.dma_start(x_plane[g, j][:], x_rows[g, j])
 
         def load_w(s, g):
-            w_raw[s, g] = tile(f"wraw{s}{g}", [P, PACK, H], F32)
+            w_raw[s, g] = tile(f"w_raw{s}{g}", [P, PACK, H], F32)
             nc.sync.dma_start(w_raw[s, g][:], (w1, w2)[s].rearrange("(g p j) c -> g p j c", p=P, j=PACK)[g])
 
         load_x(0, 0)
@@ -59,186 +67,214 @@ def tile_picked_bev_max_e_kernel(tc, xT, w1, w2, w3_words, w3_scales, offs, near
             load_x(0, j)
         load_x(1, 0)
         load_x(1, 1)
-        load_w(0, 0)
+        load_w(NEAR, 0)
         load_x(1, 2)
         load_x(1, 3)
-        load_w(0, 1)
+        load_w(NEAR, 1)
         nc.sync.dma_start(near_sb[:], near)
-        load_w(1, 0)
-        load_w(1, 1)
+        load_w(FAR, 0)
+        load_w(FAR, 1)
         nc.sync.dma_start(far_sb[:], far)
-        w3_sb = tile("w3_sb", [P, 2 * N], U8)
-        nc.sync.dma_start(w3_sb[:].bitcast(I32), w3_words[0].bitcast(I32))
+        w3_codes = tile("w3_codes", [P, 2 * N], U8)
+        nc.sync.dma_start(w3_codes[:].bitcast(I32), w3_words[0].bitcast(I32))
         w3_scale = tile("w3_scale", [P, N], U8)
         nc.gpsimd.memset(w3_scale[:], 0)
-        for q in range(4):
+        for q in range(P // 32):
             nc.sync.dma_start(w3_scale[32 * q : 32 * q + 4, :].bitcast(I32), w3_scales[0, 4 * q : 4 * q + 4, :].bitcast(I32))
 
+        ident = tile("ident", [P, P], F32)
+        make_identity(nc, ident[:])
+
         cell_map = {}
-        for s in range(2):
+        for s in SENSORS:
             for t in range(PACK):
                 cell_map[s, t] = tile(f"map{s}{t}", [P, S], F32)
-                if s == 0 and t < 3:
+                if PACK * s + t < MAPS_CLEARED_BY_VECTOR:
                     nc.vector.memset(cell_map[s, t][:], 0.0)
                 else:
-                    nc.scalar.activation(cell_map[s, t][:], cell_map[0, 0][:], RELU)
+                    nc.scalar.activation(cell_map[s, t][:], cell_map[NEAR, 0][:], RELU)
 
-        def quantize(name, woven, width, tag=None):
-            codes = tile(name + "_codes", [P, width], U32, tag)
-            scales = tile(name + "_scales", [P, width], U8)
+        def quantize(name, woven, words, after=None):
+            codes = tile(name + "_codes", [P, words], U32, after)
+            scales = tile(name + "_scales", [P, words], U8)
             nc.vector.quantize_mx(out=codes[:].bitcast(FP8X4), scales=scales[:], in_=woven)
             return codes, scales
 
-        def weave(engine_copy, dst, src):
-            engine_copy(dst.rearrange("p (c i) j -> p c j i", i=4), src.rearrange("p j (c i) -> p c j i", i=4))
+        def flat(woven):
+            return woven.rearrange("p c j -> p (c j)")
 
-        def weave_pair(engine_copy, dst, src):
-            engine_copy(dst, src.rearrange("p j c -> p c j"))
+        def weave_pair(copy, dst, src):
+            copy(dst, src.rearrange("p j c -> p c j"))
 
-        def weave_w(engine_copy, dst, src):
-            engine_copy(
-                dst.rearrange("p t (a i) j -> p a j i t", i=2),
-                src.rearrange("p j (a i t) -> p a j i t", i=2, t=PACK),
+        x_mx, w_mx = {}, {}
+
+        def quantize_w(s, g, first_tile, tiles, woven):
+            codes, scales = quantize(f"w_mx{s}{g}{first_tile}", woven, tiles * P)
+            for t in range(tiles):
+                cols = slice(t * P, (t + 1) * P)
+                w_mx[s, g, first_tile + t] = (codes[:, cols], scales[:, cols])
+
+        def prepare_w(s, woven):
+            nc.scalar.copy(
+                woven.rearrange("p (t a i j) -> p a j i t", t=PACK, i=2, j=PACK),
+                w_raw[s, 0][:].rearrange("p j (a i t) -> p a j i t", i=2, t=PACK),
             )
+            quantize_w(s, 0, 0, PACK, woven)
 
-        x_woven = {(s, 0): tile(f"xw{s}0", [P, V, PACK], BF16) for s in range(2)}
-        flat = lambda woven: woven[:].rearrange("p c j -> p (c j)")
-        xq, wq = {}, {}
+        def prepare_w_half(s, u, woven):
+            src = w_raw[s, 1][:].rearrange("p j (m t) -> p m t j", t=PACK)[:, :, 2 * u : 2 * u + 2, :]
+            nc.scalar.copy(woven.rearrange("p (t m j) -> p m t j", t=2, j=PACK), src)
+            quantize_w(s, 1, 2 * u, 2, woven)
 
+        x_woven = {(s, 0): tile(f"x_woven{s}0", [P, V, PACK], BF16)[:] for s in SENSORS}
         picked0 = tile("picked0", [P, PACK, S], BF16)
         for j in range(PACK):
             nc.vector.tensor_copy(picked0[:, j, :], x_plane[0, j][:].indirect(offs_sb[:]))
             if j % 2:
-                for s in range(2):
-                    weave_pair(nc.scalar.copy, x_woven[s, 0][:, :, j - 1 : j + 1], picked0[:, j - 1 : j + 1, s * V : (s + 1) * V])
-        picked1 = tile("picked1", [P, PACK, S], BF16)
-        for j in range(2):
-            nc.vector.tensor_copy(picked1[:, j, :], x_plane[1, j][:].indirect(offs_sb[:]))
-            xq[j, 0] = quantize(f"xq{j}0", flat(x_woven[j, 0]), V, f"x1{j}")
-        w_woven = {(s, g): tile(f"ww{s}{g}", [P, PACK, P, PACK], BF16) for s, g in ((0, 0),)}
-        wflat = lambda woven: woven.rearrange("p t m j -> p (t m j)")
-        weave_w(nc.scalar.copy, w_woven[0, 0][:], w_raw[0, 0][:])
-        far_offs = offs_sb[:, LIST_COLS : 2 * LIST_COLS]
-        wq[0, 0] = quantize("wq00", wflat(w_woven[0, 0][:]), H)
-        x12_bf16 = tile("x12_bf16", [P, T], BF16, tag="ww00")
-        nc.gpsimd.tensor_scalar(x12_bf16[:], x_plane[1, 2][:], 1.0, 0.0, MULT, ADD)
-        x_woven1 = tile("xw1", [P, 2, V, PACK], BF16, tag="wraw00")
-        for s in range(2):
-            x_woven[s, 1] = x_woven1[:, s]
-            weave_pair(nc.scalar.copy, x_woven[s, 1][:, :, 0:2], picked1[:, 0:2, s * V : (s + 1) * V])
-        for j in range(2, PACK):
-            nc.vector.tensor_copy(x_woven[0, 1][:, :, j], x_plane[1, j][:].indirect(offs_sb[:, 0:LIST_COLS]))
-        xq[0, 1] = quantize("xq01", flat(x_woven[0, 1]), V)
+                for s in SENSORS:
+                    weave_pair(nc.scalar.copy, x_woven[s, 0][:, :, j - 1 : j + 1], picked0[:, j - 1 : j + 1, pillars_of[s]])
 
-        def lhs(s, g, t):
-            if g == 1:
-                codes, scales = wq[s, 1, t // 2]
-                t = t % 2
-            else:
-                codes, scales = wq[s, g]
-            return codes[:, t * P : (t + 1) * P].bitcast(FP8X4), scales[:, t * P : (t + 1) * P]
+        picked1 = tile("picked1", [P, PACK, S], BF16)
+        for s in SENSORS:
+            nc.vector.tensor_copy(picked1[:, s, :], x_plane[1, s][:].indirect(offs_sb[:]))
+            x_mx[s, 0] = quantize(f"x_mx{s}0", flat(x_woven[s, 0]), V, after=f"x1{s}")
+        w1_woven0 = tile("w1_woven0", [P, PACK * H], BF16)
+        prepare_w(NEAR, w1_woven0[:])
+        x12_rounded = tile("x12_rounded", [P, T], BF16, after="w1_woven0")
+        nc.gpsimd.tensor_scalar(x12_rounded[:], x_plane[1, 2][:], 1.0, 0.0, MULT, ADD)
+        x_woven1 = tile("x_woven1", [P, 2, V, PACK], BF16, after="w_raw00")
+        for s in SENSORS:
+            x_woven[s, 1] = x_woven1[:, s]
+            weave_pair(nc.scalar.copy, x_woven[s, 1][:, :, 0:2], picked1[:, 0:2, pillars_of[s]])
+        for j in range(2, PACK):
+            nc.vector.tensor_copy(x_woven[NEAR, 1][:, :, j], x_plane[1, j][:].indirect(near_pillars))
+        x_mx[NEAR, 1] = quantize("x_mx01", flat(x_woven[NEAR, 1]), V)
 
         acc = {}
 
         def product(s, g, t):
             if g == 0:
-                acc[s, t] = psum.tile([P, V], F32, name=f"acc{s}{t}", tag=f"bank{4 * s + t}")
-            w_codes, w_scales = lhs(s, g, t)
-            x_codes, x_scales = xq[s, g]
-            nc.tensor.matmul_mx(out=acc[s, t][:], lhsT=w_codes, lhsT_scale=w_scales, rhs=x_codes[:].bitcast(FP8X4),
-                                rhs_scale=x_scales[:], start=(g == 0), stop=(g == 1))
+                acc[s, t] = psum.tile([P, V], F32, name=f"acc{s}{t}", tag=f"bank{PACK * s + t}")
+            w_codes, w_scales = w_mx[s, g, t]
+            x_codes, x_scales = x_mx[s, g]
+            nc.tensor.matmul_mx(
+                out=acc[s, t][:], lhsT=w_codes.bitcast(FP8X4), lhsT_scale=w_scales,
+                rhs=x_codes[:].bitcast(FP8X4), rhs_scale=x_scales[:], start=(g == 0), stop=(g == 1),
+            )
 
-        def scatter(s, t, tag=None, part=slice(0, V)):
-            staged = tile(f"staged{s}{t}_{part.start}", [P, part.stop - part.start], F32, tag)
-            if s == 0:
-                nc.scalar.activation(staged[:], acc[s, t][:, part], RELU)
+        def scatter(s, t, after=None):
+            staged = tile(f"staged{s}{t}", [P, V], F32, after)
+            if s == NEAR:
+                nc.scalar.activation(staged[:], acc[s, t][:], RELU)
+            elif t == TURNED_PLANE:
+                nc.scalar.activation(staged[:], acc[s, t][:], COPY, scale=-1.0)
             else:
-                nc.scalar.copy(staged[:], acc[s, t][:, part])
-            nc.vector.tensor_copy(cell_map[s, t][:].indirect(cells_of[s][:, part.start // 16 : part.stop // 16]), staged[:])
+                nc.scalar.copy(staged[:], acc[s, t][:])
+            nc.vector.tensor_copy(cell_map[s, t][:].indirect(cells_of[s][:]), staged[:])
 
         for t in range(PACK):
-            product(0, 0, t)
+            product(NEAR, 0, t)
+        prepare_w_half(NEAR, 0, picked1[:, 3, :])
+        product(NEAR, 1, 0)
+        nc.vector.tensor_copy(picked1[:, 3, pillars_of[FAR]], x_plane[1, 3][:].indirect(far_pillars))
+        scatter(NEAR, 0)
+        product(NEAR, 1, 1)
+        prepare_w_half(NEAR, 1, picked1[:, 2, :])
+        product(NEAR, 1, 2)
+        product(NEAR, 1, 3)
+        scatter(NEAR, 1)
 
-        def weave_w_half(s, u, dst):
-            src = w_raw[s, 1][:].rearrange("p j (m t) -> p m t j", t=PACK)[:, :, 2 * u : 2 * u + 2, :]
-            nc.scalar.copy(dst.rearrange("p (t m j) -> p m t j", t=2, j=PACK), src)
-            wq[s, 1, u] = quantize(f"wq{s}1{u}", dst, 2 * P)
-
-        weave_w_half(0, 0, picked1[:, 3, :])
-        product(0, 1, 0)
-        nc.vector.tensor_copy(picked1[:, 3, V:S], x_plane[1, 3][:].indirect(far_offs))
-        scatter(0, 0)
-        product(0, 1, 1)
-        weave_w_half(0, 1, picked1[:, 2, :])
-        product(0, 1, 2)
-        product(0, 1, 3)
-        scatter(0, 1)
-        nc.scalar.activation(picked1[:, 2, V:S], x12_bf16[:].indirect(far_offs), COPY)
-        weave_pair(nc.scalar.copy, x_woven[1, 1][:, :, 2:4], picked1[:, 2:4, V:S])
-        xq[1, 1] = quantize("xq11", flat(x_woven[1, 1]), V)
-        first_half = tile("ww110", [P, 2 * V], BF16, tag="ww00")
-        weave_w_half(1, 0, first_half[:])
-        w_woven[1, 0] = tile("ww10", [P, PACK, P, PACK], BF16, tag="picked1")
-        weave_w(nc.scalar.copy, w_woven[1, 0][:], w_raw[1, 0][:])
-        wq[1, 0] = quantize("wq10", wflat(w_woven[1, 0][:]), H)
+        nc.scalar.activation(picked1[:, 2, pillars_of[FAR]], x12_rounded[:].indirect(far_pillars), COPY)
+        weave_pair(nc.scalar.copy, x_woven[FAR, 1][:, :, 2:4], picked1[:, 2:4, pillars_of[FAR]])
+        x_mx[FAR, 1] = quantize("x_mx11", flat(x_woven[FAR, 1]), V)
+        w2_woven1_low = tile("w2_woven1_low", [P, 2 * H], BF16, after="w1_woven0")
+        prepare_w_half(FAR, 0, w2_woven1_low[:])
+        w2_woven0 = tile("w2_woven0", [P, PACK * H], BF16, after="picked1")
+        prepare_w(FAR, w2_woven0[:])
         for t in range(2):
-            product(1, 0, t)
-            product(1, 1, t)
-        scatter(0, 2, tag="wraw10")
-        second_half = tile("ww111", [P, 2 * V], BF16, tag="picked1")
-        weave_w_half(1, 1, second_half[:])
+            product(FAR, 0, t)
+            product(FAR, 1, t)
+        scatter(NEAR, 2, after="w_raw10")
+        w2_woven1_high = tile("w2_woven1_high", [P, 2 * H], BF16, after="picked1")
+        prepare_w_half(FAR, 1, w2_woven1_high[:])
         for t in range(2, PACK):
-            product(1, 0, t)
-            product(1, 1, t)
-
-        halves = [slice(0, V), slice(V, S)]
-        z_low = tile("z_low", [P, 2, S], BF16)
-
-        def join(dst, t, cols):
-            nc.vector.tensor_tensor(dst, cell_map[0, t][:, cols], cell_map[1, t][:, cols], MAX)
-
-        work = {}
-        work_tag = {(0, 0): "x02", (0, 1): "picked0", (1, 0): "x12", (1, 1): "x03", (2, 1): "x13"}
-        diff_tag = {(0, 0): "xw00", (0, 1): "xw10", (1, 0): "x02", (1, 1): "xw10", (2, 1): "x12"}
-
-        def excess(t, h):
-            diff = tile(f"diff{t}{h}", [P, V], F32, tag=diff_tag[t, h])
-            work[t, h] = tile(f"work{t}{h}", [P, V], F32, tag=work_tag[t, h])
-            nc.gpsimd.tensor_tensor(diff[:], cell_map[1, t][:, halves[h]], cell_map[0, t][:, halves[h]], SUB)
-            nc.scalar.activation(work[t, h][:], diff[:], RELU)
-
-        def add_back(dst, t, h):
-            nc.gpsimd.tensor_tensor(dst, work[t, h][:], cell_map[0, t][:, halves[h]], ADD)
-
+            product(FAR, 0, t)
+            product(FAR, 1, t)
         for t in range(PACK):
-            scatter(1, t)
-        for t in range(2):
+            scatter(FAR, t)
+
+        halves = (slice(0, HALF), slice(HALF, S))
+        z_rows = tile("z_rows", [P, 6, HALF], BF16)
+        row_of = ((4, 5, 1, 2), (2, 3, 0, 3))
+
+        def z_plane(t, h):
+            return z_rows[:, row_of[h][t], :]
+
+        def z_pair(t, h):
+            first, second = row_of[h][t], row_of[h][t + 1]
+            return z_rows[:, first : second + 1 : second - first, :]
+
+        def excess_on_gpsimd(t, diff, buffers):
+            excess = [tile(f"excess{t}{h}", [P, HALF], F32, buffers[h]) for h in range(2)]
             for h in range(2):
-                excess(t, h)
-            add_back(z_low[:, t, halves[0]], t, 0)
-            add_back(z_low[:, t, halves[1]], t, 1)
-            if t == 0:
-                scatter(0, 3, tag="picked0")
-        z_high_both = tile("z_high", [P, 2, 2, V], BF16, tag="x03")
-        z_high = [z_high_both[:, h] for h in range(2)]
-        z_woven = [tile(f"z_woven{h}", [P, V, PACK], BF16, tag=f"x0{h}") for h in range(2)]
+                nc.gpsimd.tensor_tensor(diff[:, halves[h]], cell_map[FAR, t][:, halves[h]], cell_map[NEAR, t][:, halves[h]], SUB)
+                nc.scalar.activation(excess[h][:], diff[:, halves[h]], RELU)
+            return excess
+
+        def turned_sum(name, bank, terms):
+            total = psum.tile([P, HALF], F32, name=name, tag=f"bank{bank}")
+            for b in range(HALF // P):
+                block = slice(b * P, (b + 1) * P)
+                for n, term in enumerate(terms):
+                    nc.tensor.matmul(total[:, block], term[:, block], ident[:], start=(n == 0), stop=(n == len(terms) - 1), is_transpose=True)
+            return total
+
+        near_map, minus_far_map = cell_map[NEAR, TURNED_PLANE], cell_map[FAR, TURNED_PLANE]
+        second_half_first = (1, 0)
+        near_turned = tile("near_turned", [P, S], F32)
+        for n, h in enumerate(second_half_first):
+            nc.scalar.copy(near_turned[:, halves[h]], turned_sum(f"near_psum{h}", 4 + n, [near_map[:, halves[h]]])[:])
+
+        diff0 = tile("diff0", [P, S], F32, after="x00")
+        excess0 = excess_on_gpsimd(0, diff0, ("x02", "picked0"))
         for h in range(2):
-            weave_pair(nc.scalar.copy, z_woven[h][:, :, 0:2], z_low[:, :, halves[h]])
-        for h in (1, 0):
-            join(z_high[h][:, 0, :], 2, halves[h])
-            join(z_high[h][:, 1, :], 3, halves[h])
+            nc.gpsimd.tensor_tensor(z_plane(0, h), excess0[h][:], cell_map[NEAR, 0][:, halves[h]], ADD)
+
+        scatter(NEAR, 3, after="x02")
+
+        excess_turned = [tile("excess_turned0", [P, HALF], F32), tile("excess_turned1", [P, HALF], F32, after="x00")]
+        for n, h in enumerate(second_half_first):
+            a_minus_e = turned_sum(f"gap_psum{h}", 4 + n, [minus_far_map[:, halves[h]], near_map[:, halves[h]]])
+            nc.scalar.activation(excess_turned[h][:], a_minus_e[:], RELU, scale=-1.0)
+        for h in second_half_first:
+            joined = turned_sum(f"joined_psum{h}", h, [near_turned[:, halves[h]], excess_turned[h][:]])
+            nc.scalar.copy(z_plane(TURNED_PLANE, h), joined[:])
+
+        diff2 = tile("diff2", [P, S], F32, after="picked0")
+        excess2 = excess_on_gpsimd(2, diff2, ("x12", "x00"))
         for h in range(2):
+            nc.gpsimd.tensor_tensor(z_plane(2, h), excess2[h][:], cell_map[NEAR, 2][:, halves[h]], ADD)
+
+        z_woven = [tile(f"z_woven{h}", [P, HALF, PACK], BF16, ("x00", "picked0")[h]) for h in range(2)]
+        for h in second_half_first:
+            weave_pair(nc.scalar.copy, z_woven[h][:, :, 0:2], z_pair(0, h))
+        for h in range(2):
+            nc.vector.tensor_tensor(z_plane(3, h), cell_map[NEAR, 3][:, halves[h]], cell_map[FAR, 3][:, halves[h]], MAX)
+        for h, copy in enumerate((nc.vector.tensor_copy, nc.scalar.copy)):
             for u in range(2):
-                cols = slice(u * V // 2, (u + 1) * V // 2)
-                weave_pair((nc.vector.tensor_copy, nc.scalar.copy)[h], z_woven[h][:, cols, 2:4], z_high[h][:, :, cols])
-        quarter = V // 2
-        result = tile("result", [P, S], F32, tag="x03")
-        for n, (h, u) in enumerate(((0, 0), (0, 1), (1, 0), (1, 1))):
-            z_in = z_woven[h][:, u * quarter : (u + 1) * quarter, :].rearrange("p c j -> p (c j)")
-            z_codes, z_scales = quantize(f"zq{n}", z_in, quarter)
-            res = psum.tile([P, quarter], F32, name=f"res{n}", tag=f"bank{n}")
-            nc.tensor.matmul_mx(out=res[:], lhsT=w3_sb[:].bitcast(FP4X4), lhsT_scale=w3_scale[:], rhs=z_codes[:].bitcast(FP8X4),
-                                rhs_scale=z_scales[:], start=True, stop=True)
-            cols = slice(n * quarter, (n + 1) * quarter)
-            (nc.scalar.copy, nc.vector.tensor_copy)[n == PACK - 1](result[:, cols], res[:])
+                cols = slice(u * QUARTER, (u + 1) * QUARTER)
+                weave_pair(copy, z_woven[h][:, cols, 2:4], z_pair(2, h)[:, :, cols])
+
+        result = tile("result", [P, S], F32, after="z_rows")
+        for n in range(S // QUARTER):
+            h, u = divmod(n, 2)
+            z_codes, z_scales = quantize(f"z_mx{n}", flat(z_woven[h][:, u * QUARTER : (u + 1) * QUARTER, :]), QUARTER)
+            out_psum = psum.tile([P, QUARTER], F32, name=f"out_psum{n}", tag=f"bank{n}")
+            nc.tensor.matmul_mx(
+                out=out_psum[:], lhsT=w3_codes[:].bitcast(FP4X4), lhsT_scale=w3_scale[:],
+                rhs=z_codes[:].bitcast(FP8X4), rhs_scale=z_scales[:], start=True, stop=True,
+            )
+            cols = slice(n * QUARTER, (n + 1) * QUARTER)
+            copy = nc.vector.tensor_copy if n == S // QUARTER - 1 else nc.scalar.copy
+            copy(result[:, cols], out_psum[:])
             nc.sync.dma_start(out[:, cols], result[:, cols])

from contextlib import ExitStack

import concourse.mybir as mybir
from concourse.masks import make_identity

K, T, S, H, N, V = 1024, 2048, 1024, 512, 128, 512
FLOPS = 2 * (2 * K * H * V + H * N * S)

F32 = mybir.dt.float32
BF16 = mybir.dt.bfloat16
I32 = mybir.dt.int32
U32 = mybir.dt.uint32
U16 = mybir.dt.uint16
U8 = mybir.dt.uint8
FP8X4 = mybir.dt.float8_e4m3fn_x4
FP4X4 = mybir.dt.float4_e2m1fn_x4
MAX = mybir.AluOpType.max
ADD = mybir.AluOpType.add
MULT = mybir.AluOpType.mult
SUB = mybir.AluOpType.subtract
COPY = mybir.ActivationFunctionType.Copy
RELU = mybir.ActivationFunctionType.Relu

P = 128
PACK = 4
NEAR, FAR = 0, 1
SENSORS = (NEAR, FAR)
LIST_COLS = V // 16
HALF = S // 2
QUARTER = S // 4
MAPS_CLEARED_BY_VECTOR = 3
TURNED_PLANE = 1


def tile_picked_bev_max_e_kernel(tc, xT, w1, w2, w3_words, w3_scales, offs, near, far, out):
    nc = tc.nc
    with ExitStack() as ctx:
        lists = ctx.enter_context(tc.tile_pool(name="lists", bufs=1))
        sb = ctx.enter_context(tc.tile_pool(name="sb", bufs=1))
        psum = ctx.enter_context(tc.psum_pool(name="psum", bufs=1))

        def tile(name, shape, dtype, after=None):
            return sb.tile(shape, dtype, name=name, tag=after or name, align_bytes=64)

        offs_sb = lists.tile([P, S // 16], U16, name="offs_sb")
        near_sb = lists.tile([P, LIST_COLS], U16, name="near_sb")
        far_sb = lists.tile([P, LIST_COLS], U16, name="far_sb")
        cells_of = (near_sb, far_sb)
        near_pillars = offs_sb[:, 0:LIST_COLS]
        far_pillars = offs_sb[:, LIST_COLS : 2 * LIST_COLS]
        pillars_of = (slice(0, V), slice(V, 2 * V))

        x_rows = xT.rearrange("(g p j) t -> g j p t", p=P, j=PACK)
        x_plane, w_raw = {}, {}

        def load_x(g, j):
            x_plane[g, j] = tile(f"x{g}{j}", [P, T], F32)
            nc.sync.dma_start(x_plane[g, j][:], x_rows[g, j])

        def load_w(s, g):
            w_raw[s, g] = tile(f"w_raw{s}{g}", [P, PACK, H], F32)
            nc.sync.dma_start(w_raw[s, g][:], (w1, w2)[s].rearrange("(g p j) c -> g p j c", p=P, j=PACK)[g])

        load_x(0, 0)
        nc.sync.dma_start(offs_sb[:], offs)
        for j in range(1, PACK):
            load_x(0, j)
        load_x(1, 0)
        load_x(1, 1)
        load_w(NEAR, 0)
        load_x(1, 2)
        load_x(1, 3)
        load_w(NEAR, 1)
        nc.sync.dma_start(near_sb[:], near)
        load_w(FAR, 0)
        load_w(FAR, 1)
        nc.sync.dma_start(far_sb[:], far)
        w3_codes = tile("w3_codes", [P, 2 * N], U8)
        nc.sync.dma_start(w3_codes[:].bitcast(I32), w3_words[0].bitcast(I32))
        w3_scale = tile("w3_scale", [P, N], U8)
        nc.gpsimd.memset(w3_scale[:], 0)
        for q in range(P // 32):
            nc.sync.dma_start(w3_scale[32 * q : 32 * q + 4, :].bitcast(I32), w3_scales[0, 4 * q : 4 * q + 4, :].bitcast(I32))

        ident = tile("ident", [P, P], F32)
        make_identity(nc, ident[:])

        cell_map = {}
        for s in SENSORS:
            for t in range(PACK):
                cell_map[s, t] = tile(f"map{s}{t}", [P, S], F32)
                if PACK * s + t < MAPS_CLEARED_BY_VECTOR:
                    nc.vector.memset(cell_map[s, t][:], 0.0)
                else:
                    nc.scalar.activation(cell_map[s, t][:], cell_map[NEAR, 0][:], RELU)

        def quantize(name, woven, words, after=None):
            codes = tile(name + "_codes", [P, words], U32, after)
            scales = tile(name + "_scales", [P, words], U8)
            nc.vector.quantize_mx(out=codes[:].bitcast(FP8X4), scales=scales[:], in_=woven)
            return codes, scales

        def flat(woven):
            return woven.rearrange("p c j -> p (c j)")

        def weave_pair(copy, dst, src):
            copy(dst, src.rearrange("p j c -> p c j"))

        x_mx, w_mx = {}, {}

        def quantize_w(s, g, first_tile, tiles, woven):
            codes, scales = quantize(f"w_mx{s}{g}{first_tile}", woven, tiles * P)
            for t in range(tiles):
                cols = slice(t * P, (t + 1) * P)
                w_mx[s, g, first_tile + t] = (codes[:, cols], scales[:, cols])

        def prepare_w(s, woven):
            nc.scalar.copy(
                woven.rearrange("p (t a i j) -> p a j i t", t=PACK, i=2, j=PACK),
                w_raw[s, 0][:].rearrange("p j (a i t) -> p a j i t", i=2, t=PACK),
            )
            quantize_w(s, 0, 0, PACK, woven)

        def prepare_w_half(s, u, woven):
            src = w_raw[s, 1][:].rearrange("p j (m t) -> p m t j", t=PACK)[:, :, 2 * u : 2 * u + 2, :]
            nc.scalar.copy(woven.rearrange("p (t m j) -> p m t j", t=2, j=PACK), src)
            quantize_w(s, 1, 2 * u, 2, woven)

        x_woven = {(s, 0): tile(f"x_woven{s}0", [P, V, PACK], BF16)[:] for s in SENSORS}
        picked0 = tile("picked0", [P, PACK, S], BF16)
        for j in range(PACK):
            nc.vector.tensor_copy(picked0[:, j, :], x_plane[0, j][:].indirect(offs_sb[:]))
            if j % 2:
                for s in SENSORS:
                    weave_pair(nc.scalar.copy, x_woven[s, 0][:, :, j - 1 : j + 1], picked0[:, j - 1 : j + 1, pillars_of[s]])

        picked1 = tile("picked1", [P, PACK, S], BF16)
        for s in SENSORS:
            nc.vector.tensor_copy(picked1[:, s, :], x_plane[1, s][:].indirect(offs_sb[:]))
            x_mx[s, 0] = quantize(f"x_mx{s}0", flat(x_woven[s, 0]), V, after=f"x1{s}")
        w1_woven0 = tile("w1_woven0", [P, PACK * H], BF16)
        prepare_w(NEAR, w1_woven0[:])
        x12_rounded = tile("x12_rounded", [P, T], BF16, after="w1_woven0")
        nc.gpsimd.tensor_scalar(x12_rounded[:], x_plane[1, 2][:], 1.0, 0.0, MULT, ADD)
        x_woven1 = tile("x_woven1", [P, 2, V, PACK], BF16, after="w_raw00")
        for s in SENSORS:
            x_woven[s, 1] = x_woven1[:, s]
            weave_pair(nc.scalar.copy, x_woven[s, 1][:, :, 0:2], picked1[:, 0:2, pillars_of[s]])
        for j in range(2, PACK):
            nc.vector.tensor_copy(x_woven[NEAR, 1][:, :, j], x_plane[1, j][:].indirect(near_pillars))
        x_mx[NEAR, 1] = quantize("x_mx01", flat(x_woven[NEAR, 1]), V)

        acc = {}

        def product(s, g, t):
            if g == 0:
                acc[s, t] = psum.tile([P, V], F32, name=f"acc{s}{t}", tag=f"bank{PACK * s + t}")
            w_codes, w_scales = w_mx[s, g, t]
            x_codes, x_scales = x_mx[s, g]
            nc.tensor.matmul_mx(
                out=acc[s, t][:], lhsT=w_codes.bitcast(FP8X4), lhsT_scale=w_scales,
                rhs=x_codes[:].bitcast(FP8X4), rhs_scale=x_scales[:], start=(g == 0), stop=(g == 1),
            )

        def scatter(s, t, after=None):
            staged = tile(f"staged{s}{t}", [P, V], F32, after)
            if s == NEAR:
                nc.scalar.activation(staged[:], acc[s, t][:], RELU)
            elif t == TURNED_PLANE:
                nc.scalar.activation(staged[:], acc[s, t][:], COPY, scale=-1.0)
            else:
                nc.scalar.copy(staged[:], acc[s, t][:])
            nc.vector.tensor_copy(cell_map[s, t][:].indirect(cells_of[s][:]), staged[:])

        for t in range(PACK):
            product(NEAR, 0, t)
        prepare_w_half(NEAR, 0, picked1[:, 3, :])
        product(NEAR, 1, 0)
        nc.vector.tensor_copy(picked1[:, 3, pillars_of[FAR]], x_plane[1, 3][:].indirect(far_pillars))
        scatter(NEAR, 0)
        product(NEAR, 1, 1)
        prepare_w_half(NEAR, 1, picked1[:, 2, :])
        product(NEAR, 1, 2)
        product(NEAR, 1, 3)
        scatter(NEAR, 1)

        nc.scalar.activation(picked1[:, 2, pillars_of[FAR]], x12_rounded[:].indirect(far_pillars), COPY)
        weave_pair(nc.scalar.copy, x_woven[FAR, 1][:, :, 2:4], picked1[:, 2:4, pillars_of[FAR]])
        x_mx[FAR, 1] = quantize("x_mx11", flat(x_woven[FAR, 1]), V)
        w2_woven1_low = tile("w2_woven1_low", [P, 2 * H], BF16, after="w1_woven0")
        prepare_w_half(FAR, 0, w2_woven1_low[:])
        w2_woven0 = tile("w2_woven0", [P, PACK * H], BF16, after="picked1")
        prepare_w(FAR, w2_woven0[:])
        for t in range(2):
            product(FAR, 0, t)
            product(FAR, 1, t)
        scatter(NEAR, 2, after="w_raw10")
        w2_woven1_high = tile("w2_woven1_high", [P, 2 * H], BF16, after="picked1")
        prepare_w_half(FAR, 1, w2_woven1_high[:])
        for t in range(2, PACK):
            product(FAR, 0, t)
            product(FAR, 1, t)
        for t in range(PACK):
            scatter(FAR, t)

        halves = (slice(0, HALF), slice(HALF, S))
        z_rows = tile("z_rows", [P, 6, HALF], BF16)
        row_of = ((4, 5, 1, 2), (2, 3, 0, 3))

        def z_plane(t, h):
            return z_rows[:, row_of[h][t], :]

        def z_pair(t, h):
            first, second = row_of[h][t], row_of[h][t + 1]
            return z_rows[:, first : second + 1 : second - first, :]

        def excess_on_gpsimd(t, diff, buffers):
            excess = [tile(f"excess{t}{h}", [P, HALF], F32, buffers[h]) for h in range(2)]
            for h in range(2):
                nc.gpsimd.tensor_tensor(diff[:, halves[h]], cell_map[FAR, t][:, halves[h]], cell_map[NEAR, t][:, halves[h]], SUB)
                nc.scalar.activation(excess[h][:], diff[:, halves[h]], RELU)
            return excess

        def turned_sum(name, bank, terms):
            total = psum.tile([P, HALF], F32, name=name, tag=f"bank{bank}")
            for b in range(HALF // P):
                block = slice(b * P, (b + 1) * P)
                for n, term in enumerate(terms):
                    nc.tensor.matmul(total[:, block], term[:, block], ident[:], start=(n == 0), stop=(n == len(terms) - 1), is_transpose=True)
            return total

        near_map, minus_far_map = cell_map[NEAR, TURNED_PLANE], cell_map[FAR, TURNED_PLANE]
        second_half_first = (1, 0)
        near_turned = tile("near_turned", [P, S], F32)
        for n, h in enumerate(second_half_first):
            nc.scalar.copy(near_turned[:, halves[h]], turned_sum(f"near_psum{h}", 4 + n, [near_map[:, halves[h]]])[:])

        diff0 = tile("diff0", [P, S], F32, after="x00")
        excess0 = excess_on_gpsimd(0, diff0, ("x02", "picked0"))
        for h in range(2):
            nc.gpsimd.tensor_tensor(z_plane(0, h), excess0[h][:], cell_map[NEAR, 0][:, halves[h]], ADD)

        scatter(NEAR, 3, after="x02")

        excess_turned = [tile("excess_turned0", [P, HALF], F32), tile("excess_turned1", [P, HALF], F32, after="x00")]
        for n, h in enumerate(second_half_first):
            a_minus_e = turned_sum(f"gap_psum{h}", 4 + n, [minus_far_map[:, halves[h]], near_map[:, halves[h]]])
            nc.scalar.activation(excess_turned[h][:], a_minus_e[:], RELU, scale=-1.0)
        for h in second_half_first:
            joined = turned_sum(f"joined_psum{h}", h, [near_turned[:, halves[h]], excess_turned[h][:]])
            nc.scalar.copy(z_plane(TURNED_PLANE, h), joined[:])

        diff2 = tile("diff2", [P, S], F32, after="picked0")
        excess2 = excess_on_gpsimd(2, diff2, ("x12", "x00"))
        for h in range(2):
            nc.gpsimd.tensor_tensor(z_plane(2, h), excess2[h][:], cell_map[NEAR, 2][:, halves[h]], ADD)

        z_woven = [tile(f"z_woven{h}", [P, HALF, PACK], BF16, ("x00", "picked0")[h]) for h in range(2)]
        for h in second_half_first:
            weave_pair(nc.scalar.copy, z_woven[h][:, :, 0:2], z_pair(0, h))
        for h in range(2):
            nc.vector.tensor_tensor(z_plane(3, h), cell_map[NEAR, 3][:, halves[h]], cell_map[FAR, 3][:, halves[h]], MAX)
        for h, copy in enumerate((nc.vector.tensor_copy, nc.scalar.copy)):
            for u in range(2):
                cols = slice(u * QUARTER, (u + 1) * QUARTER)
                weave_pair(copy, z_woven[h][:, cols, 2:4], z_pair(2, h)[:, :, cols])

        result = tile("result", [P, S], F32, after="z_rows")
        for n in range(S // QUARTER):
            h, u = divmod(n, 2)
            z_codes, z_scales = quantize(f"z_mx{n}", flat(z_woven[h][:, u * QUARTER : (u + 1) * QUARTER, :]), QUARTER)
            out_psum = psum.tile([P, QUARTER], F32, name=f"out_psum{n}", tag=f"bank{n}")
            nc.tensor.matmul_mx(
                out=out_psum[:], lhsT=w3_codes[:].bitcast(FP4X4), lhsT_scale=w3_scale[:],
                rhs=z_codes[:].bitcast(FP8X4), rhs_scale=z_scales[:], start=True, stop=True,
            )
            cols = slice(n * QUARTER, (n + 1) * QUARTER)
            copy = nc.vector.tensor_copy if n == S // QUARTER - 1 else nc.scalar.copy
            copy(result[:, cols], out_psum[:])
            nc.sync.dma_start(out[:, cols], result[:, cols])
